import numpy as np, ml_dtypes
CORES = [6,14,22,30,38,134,142,150,158]
N = 9
import mx_ref
NC, K = 128, 4
CNT = [[0,0,12,4,0,64,20,28,0],[4,0,0,32,16,0,72,4,0],[52,8,0,12,28,8,0,0,20],[0,48,0,0,16,4,4,24,32],[12,8,0,48,0,20,20,12,8],[8,4,36,0,48,0,4,8,20],[20,20,12,0,12,12,0,4,48],[32,8,60,20,8,0,0,0,0],[0,32,8,12,0,20,8,48,0]]
OFF = [[sum(c[:e]) for e in range(N + 1)] for c in CNT]
BF = ml_dtypes.bfloat16
def setup_inputs(rng):
    def f(*shape):
        return mx_ref.flush((rng.standard_normal(shape, dtype=np.float32) * np.exp2(rng.integers(-2, 3, shape[:-1] + (1,)))).astype(BF))
    return {"x": f(N, 128, 4 * NC), "w": f(N, 128, 512)}
def setup_inputs_blocks(rng):
    d = setup_inputs(rng)
    for k in ("x", "w"): d[k] = mx_ref.spread(d[k], rng, 4)
    return d
def setup_inputs_wide(rng):
    d = setup_inputs(rng)
    for k in ("x", "w"): d[k] = mx_ref.flush((d[k].astype(np.float32) * np.exp2(rng.integers(-8, 9, (N, 1, 1))).astype(np.float32)).astype(BF))
    return d
def setup_inputs_zeros(rng):
    d = setup_inputs(rng); v = d["x"].reshape(N, 128, -1, 4).copy()
    v[np.broadcast_to((rng.random((N, 1, v.shape[2], 1)) < 0.33), v.shape)] = 0
    d["x"] = v.reshape(d["x"].shape)
    return d
def reference(x, w):
    y = np.zeros((N, 128, K * NC), np.float32)
    for e in range(N):
        t = np.concatenate([x[j][:, 4 * OFF[j][(e - k) % N]:4 * OFF[j][(e - k) % N + 1]] for k in range(K) for j in range(N)], axis=1)
        y[e] = mx_ref.matmul(mx_ref.quantize(w[e]), mx_ref.quantize(t))
    return {"y": y}

@@ -1,0 +1,218 @@
+from concourse.bass import DstId, RemoteDMATransfer
+from concourse.mybir import dt, ActivationFunctionType
+
+SCRATCH = {
+    "xt": ("sbuf", [128, 1024], "bfloat16"),
+    "wt": ("sbuf", [128, 512], "bfloat16"),
+    "xq": ("sbuf", [128, 256], "float8_e4m3fn_x4"),
+    "xs": ("sbuf", [128, 256], "uint8"),
+    "wq": ("sbuf", [128, 128], "float8_e4m3fn_x4"),
+    "ws": ("sbuf", [128, 128], "uint8"),
+    "rq": ("sbuf", [128, 128], "float8_e4m3fn_x4"),
+    "rs": ("sbuf", [128, 128], "uint8"),
+    "bq": ("sbuf", [128, 512], "float8_e4m3fn_x4"),
+    "bs": ("sbuf", [128, 512], "uint8"),
+    "cq": ("sbuf", [128, 512], "float8_e4m3fn_x4"),
+    "cs": ("sbuf", [128, 512], "uint8"),
+    "ys": ("sbuf", [128, 512], "float32"),
+    "p0": ("psum", [128, 512], "float32"),
+    "p1": ("psum", [128, 512], "float32"),
+    "p2": ("psum", [128, 512], "float32"),
+    "p3": ("psum", [128, 512], "float32"),
+    "p4": ("psum", [128, 512], "float32"),
+}
+SEMAPHORES = ["ldx", "ldw", "qx", "qw", "sent", "ra", "bin", "cin", "m0", "m1", "m2", "m3", "m4", "lo", "hi", "st"]
+K, NC, WORLD = 4, 128, 256
+
+
+def bits(mask):
+    return [1 << b for b in range(16) if mask >> b & 1]
+
+
+def share(src, dsts, topo):
+    masks = {d: bits(topo.mask(src, d)) for d in dsts}
+    few = min(len(m) for m in masks.values())
+    n = sum(1 for m in masks.values() if len(m) == few)
+    per = 1
+    while 2 * per * n <= few:
+        per *= 2
+    used, out = set(), {}
+    for d in sorted(dsts, key=lambda c: len(masks[c])):
+        free = [b for b in masks[d] if b not in used][:per]
+        used.update(free)
+        out[d] = sum(free)
+    return out
+
+
+def plan(T, topo):
+    cnt, cores = T.tables["CNT"], T.cores
+    n = len(cores)
+    host = [topo.host(c) for c in cores]
+    f0 = min(e for e in range(n) if host[e] != host[0]) - (K - 1)
+    seq = [(f0 + i) % n for i in range(n + K - 1)]
+    at = {e: next(i for i in range(n) if seq[i:i + K] == [(e - K + 1 + k) % n for k in range(K)]) for e in range(n)}
+    P = {"n": n, "f0": f0, "seq": seq, "at": at, "host": host}
+    pos = [[sum(cnt[j][f] for f in seq[:i]) for i in range(len(seq) + 1)] for j in range(n)]
+    P["pos"] = pos
+    win = [[(pos[j][at[e]], pos[j][at[e] + K]) for e in range(n)] for j in range(n)]
+    P["win"] = win
+    live = lambda j, e: j != e and win[j][e][1] > win[j][e][0]
+    P["inside"] = [[e for e in range(n) if host[e] == host[j] and live(j, e)] for j in range(n)]
+    P["across"] = [[e for e in range(n) if host[e] != host[j] and live(j, e)] for j in range(n)]
+    P["run"] = [(min(win[j][e][0] for e in P["across"][j]), max(win[j][e][1] for e in P["across"][j])) for j in range(n)]
+    width = {}
+    for kind in ("inside", "across"):
+        w = [max(win[j][e][1] - win[j][e][0] for e in P[kind][j]) for j in range(n)]
+        while True:
+            short = [[j for j in range(n) if e in P[kind][j]] for e in range(n)
+                     if sum(w[j] for j in range(n) if e in P[kind][j]) < NC]
+            if not short:
+                break
+            w[min(short[0], key=lambda j: w[j])] += 4
+        width[kind] = w
+    P["width"] = width
+    P["slot"] = {}
+    for kind in ("inside", "across"):
+        for e in range(n):
+            o, s = 0, {}
+            for j in range(n):
+                if e in P[kind][j]:
+                    s[j] = o
+                    o += width[kind][j]
+            P["slot"][kind, e] = (s, o)
+    start = {}
+    for j in range(n):
+        for e in P["inside"][j]:
+            start[j, e] = min(win[j][e][0], pos[j][-1] - width["inside"][j])
+        for e in P["across"][j]:
+            start[j, e] = min(win[j][e][0], P["run"][j][1] - width["across"][j])
+    P["start"] = start
+    taken, relay = set(), []
+    for j in range(n):
+        src = cores[j]
+        dst = [cores[e] for e in P["across"][j]]
+        by = {}
+        for c in range(WORLD):
+            if (topo.host(c) == topo.host(dst[0]) and topo.same_plane(src, c) and topo.die(c) != topo.die(src)
+                    and all(topo.may_write(c, d) for d in dst)):
+                by.setdefault(topo.chip(c), []).append(c)
+        ranked = [topo.chip(d) for d in dst]
+        chip = min((h for h in by if (topo.host(dst[0]), h) not in taken and len(by[h]) >= 2), key=lambda h: (h not in ranked, h))
+        taken.add((topo.host(dst[0]), chip))
+        relay.append(by[chip][:2])
+    P["relay"] = relay
+    arr = {}
+    for j in range(n):
+        for kind, srcs, sem in (("inside", [cores[j]] * 2, "bin"), ("across", relay[j], "cin")):
+            for s in srcs:
+                for d, m in share(s, [cores[e] for e in P[kind][j]], topo).items():
+                    arr[d, sem] = arr.get((d, sem), 0) + len(bits(m))
+    P["arr"] = arr
+    return P
+
+
+def send_windows(g, T, topo, core, P, j, kind, codes, base, sem):
+    src, dst = {("inside", True): ("xq", "bq"), ("inside", False): ("xs", "bs"),
+                ("across", True): ("rq", "cq"), ("across", False): ("rs", "cs")}[kind, codes]
+    w = P["width"][kind][j]
+    masks = share(core, [T.cores[e] for e in P[kind][j]], topo)
+    tr = []
+    for e in P[kind][j]:
+        d = T.cores[e]
+        rid, pid = topo.addr(d, core)
+        a, o = P["start"][j, e] - base, P["slot"][kind, e][0][j]
+        s, t = T[src][:, a:a + w], T[dst][:, o:o + w]
+        if codes:
+            s, t = s.bitcast(dt.uint8), t.bitcast(dt.uint8)
+        tr.append(RemoteDMATransfer(dst_ids=[DstId(rid=rid, pnc=pid)], dma_engine_mask=masks[d], remote_sem=T.sem[sem], src=s, dst=t))
+    g.remote_dma_fused(tr, local_sem=T.sem.sent)
+    return sum(len(bits(m)) for m in masks.values())
+
+
+def relay_program(g, core, T, topo, P):
+    for j in range(P["n"]):
+        if core in P["relay"][j]:
+            g.wait_ge(T.sem.ra, len(bits(topo.mask(T.cores[j], core))))
+            g.wait_ge(T.sem.sent, send_windows(g, T, topo, core, P, j, "across", core == P["relay"][j][0], P["run"][j][0], "cin"))
+
+
+def bank_views(slots, total, cost):
+    js = sorted(slots)
+    cut = min(range(1, len(js)), key=lambda c: max(sum(cost[j] for j in js[:c]), sum(cost[j] for j in js[c:])))
+    mid = slots[js[cut]]
+    return [(js[:cut], 0, max(mid, NC)), (js[cut:], min(mid, total - NC), total)]
+
+
+def rank_program(g, core, T, topo):
+    rank = T.rank_of(core)
+    P = plan(T, topo)
+    if rank is None:
+        relay_program(g, core, T, topo, P)
+        return
+    cnt, n, win = T.tables["CNT"], P["n"], P["win"]
+    pos = P["pos"][rank]
+    tail = pos[n - P["f0"]]
+    ext = pos[-1]
+    g.sync.dma_start(T.xt[:, 0:4 * tail], T.x[:, 4 * (NC - tail):4 * NC]).then_inc(T.sem.ldx, 16)
+    g.scalar.dma_start(T.xt[:, 4 * tail:4 * ext], T.x[:, 0:4 * (ext - tail)]).then_inc(T.sem.ldx, 16)
+    g.sync.dma_start(T.wt[:], T.w[:]).then_inc(T.sem.ldw, 16)
+    g.vector.wait_ge(T.sem.ldx, 32)
+    g.vector.quantize_mx(T.xq[:, 0:ext], T.xs[:, 0:ext], T.xt[:, 0:4 * ext]).then_inc(T.sem.qx, 1)
+    g.vector.wait_ge(T.sem.ldw, 16)
+    g.vector.quantize_mx(T.wq[:], T.ws[:], T.wt[:]).then_inc(T.sem.qw, 1)
+    g.wait_ge(T.sem.qx, 1)
+    sent = 0
+    a, b = P["run"][rank]
+    for to, codes in zip(P["relay"][rank], (True, False)):
+        rid, pid = topo.addr(to, core)
+        m = topo.mask(core, to)
+        if codes:
+            g.remote_dma(T.rq[:, 0:b - a].bitcast(dt.uint8), T.xq[:, a:b].bitcast(dt.uint8), T.sem.ra, T.sem.sent, pid, rid, m)
+        else:
+            g.remote_dma(T.rs[:, 0:b - a], T.xs[:, a:b], T.sem.ra, T.sem.sent, pid, rid, m)
+        sent += len(bits(m))
+    for codes in (True, False):
+        sent += send_windows(g, T, topo, core, P, rank, "inside", codes, 0, "bin")
+    g.wait_ge(T.sem.sent, sent)
+    e = rank
+    a = min(win[e][e][0], ext - NC)
+    groups = [(T.p0, T.sem.m0, "own", [e], T.xq, T.xs, a, a + NC)]
+    cost = {j: sum(max(64, cnt[j][(e - k) % n]) + 40 for k in range(K) if cnt[j][(e - k) % n]) for j in range(n)}
+    for kind, q, s, banks in (("inside", T.bq, T.bs, (1, 2)), ("across", T.cq, T.cs, (3, 4))):
+        slots, total = P["slot"][kind, e]
+        for i, (js, lo, hi) in zip(banks, bank_views(slots, total, cost)):
+            groups.append((T["p%d" % i], T.sem["m%d" % i], kind, js, q, s, lo, hi))
+    g.tensor.wait_ge(T.sem.qx, 1)
+    g.tensor.wait_ge(T.sem.qw, 1)
+    for i, (bank, sem, kind, js, q, s, lo, hi) in enumerate(groups):
+        if i == 1:
+            g.tensor.wait_ge(T.sem.bin, P["arr"][core, "bin"])
+        if i == 3:
+            g.tensor.wait_ge(T.sem.cin, P["arr"][core, "cin"])
+        g.tensor.matmul_mx(bank[:, 0:hi - lo], T.wq[:], T.ws[:], q[:, lo:hi], s[:, lo:hi], True, True).then_inc(sem, 1)
+    done = {"lo": 0, "hi": 0}
+    for i, (bank, sem, kind, js, q, s, lo, hi) in enumerate(groups):
+        on_scalar = i in (2, 4)
+        (g.scalar if on_scalar else g.vector).wait_ge(sem, 1)
+        for k in range(K):
+            f = (e - k) % n
+            for j in js:
+                c = cnt[j][f]
+                if not c:
+                    continue
+                o = win[j][e][0] + sum(cnt[j][(e - m) % n] for m in range(k + 1, K))
+                if kind != "own":
+                    o += P["slot"][kind, e][0][j] - P["start"][j, e]
+                o -= lo
+                to = k * NC + sum(cnt[i2][f] for i2 in range(j))
+                half = "lo" if k < 2 else "hi"
+                done[half] += 1
+                if on_scalar:
+                    g.scalar.activation(T.ys[:, to:to + c], bank[:, o:o + c], ActivationFunctionType.Copy).then_inc(T.sem[half], 1)
+                else:
+                    g.vector.tensor_copy(T.ys[:, to:to + c], bank[:, o:o + c]).then_inc(T.sem[half], 1)
+    g.sync.wait_ge(T.sem.lo, done["lo"])
+    g.sync.dma_start(T.y[:, 0:2 * NC], T.ys[:, 0:2 * NC]).then_inc(T.sem.st, 16)
+    g.scalar.wait_ge(T.sem.hi, done["hi"])
+    g.scalar.dma_start(T.y[:, 2 * NC:4 * NC], T.ys[:, 2 * NC:4 * NC]).then_inc(T.sem.st, 16)
+    g.sync.wait_ge(T.sem.st, 32)

@@ -2,18 +2,18 @@ from concourse.bass import DstId, RemoteDMATransfer
 from concourse.mybir import dt, ActivationFunctionType
 
 SCRATCH = {
-    "xt": ("sbuf", [128, 1024], "bfloat16"),
+    "xt": ("sbuf", [128, 512], "bfloat16"),
     "wt": ("sbuf", [128, 512], "bfloat16"),
     "xq": ("sbuf", [128, 256], "float8_e4m3fn_x4"),
     "xs": ("sbuf", [128, 256], "uint8"),
     "wq": ("sbuf", [128, 128], "float8_e4m3fn_x4"),
     "ws": ("sbuf", [128, 128], "uint8"),
-    "rq": ("sbuf", [128, 128], "float8_e4m3fn_x4"),
-    "rs": ("sbuf", [128, 128], "uint8"),
-    "bq": ("sbuf", [128, 512], "float8_e4m3fn_x4"),
-    "bs": ("sbuf", [128, 512], "uint8"),
-    "cq": ("sbuf", [128, 512], "float8_e4m3fn_x4"),
-    "cs": ("sbuf", [128, 512], "uint8"),
+    "rq": ("sbuf", [128, 256], "float8_e4m3fn_x4"),
+    "rs": ("sbuf", [128, 256], "uint8"),
+    "bq": ("sbuf", [128, 640], "float8_e4m3fn_x4"),
+    "bs": ("sbuf", [128, 640], "uint8"),
+    "cq": ("sbuf", [128, 640], "float8_e4m3fn_x4"),
+    "cs": ("sbuf", [128, 640], "uint8"),
     "ys": ("sbuf", [128, 512], "float32"),
     "p0": ("psum", [128, 512], "float32"),
     "p1": ("psum", [128, 512], "float32"),
@@ -21,198 +21,257 @@ SCRATCH = {
     "p3": ("psum", [128, 512], "float32"),
     "p4": ("psum", [128, 512], "float32"),
 }
-SEMAPHORES = ["ldx", "ldw", "qx", "qw", "sent", "ra", "bin", "cin", "m0", "m1", "m2", "m3", "m4", "lo", "hi", "st"]
+SEMAPHORES = ["ldx", "ldw", "qx", "qy", "qw", "sent", "ra", "b0", "b1", "c0", "c1", "m0", "m1", "m2", "m3", "m4",
+              "early", "f0", "f1", "f2", "f3", "st"]
 K, NC, WORLD = 4, 128, 256
+CALL, ROW, BYTE = 0.1, 0.012, 1 / 14000.
+CACHE = {}
 
 
 def bits(mask):
     return [1 << b for b in range(16) if mask >> b & 1]
 
 
-def share(src, dsts, topo):
-    masks = {d: bits(topo.mask(src, d)) for d in dsts}
-    few = min(len(m) for m in masks.values())
-    n = sum(1 for m in masks.values() if len(m) == few)
-    per = 1
-    while 2 * per * n <= few:
-        per *= 2
-    used, out = set(), {}
-    for d in sorted(dsts, key=lambda c: len(masks[c])):
-        free = [b for b in masks[d] if b not in used][:per]
-        used.update(free)
-        out[d] = sum(free)
-    return out
+def partitions(items):
+    if not items:
+        yield []
+        return
+    for rest in partitions(items[1:]):
+        yield [[items[0]]] + rest
+        for i in range(len(rest)):
+            yield rest[:i] + [[items[0]] + rest[i]] + rest[i + 1:]
+
+
+def pack(core, wins, hi, topo):
+    masks = {d: topo.mask(core, d) for d in wins}
+    few = min(len(bits(m)) for m in masks.values())
+    far = [d for d in wins if len(bits(masks[d])) == few]
+    pool = bits(masks[far[0]])
+    best = None
+    for part in partitions(sorted(wins)):
+        cost, off, on, groups = 0, 0, 0, []
+        for grp in part:
+            w = max(wins[d][1] - wins[d][0] for d in grp)
+            out = sum(1 for d in grp if d in far)
+            per = 1
+            while 2 * per * max(1, out) <= len(pool):
+                per *= 2
+            t = NC / per * (ROW + 4 * w * BYTE)
+            off += t if out else 0
+            on += t if out < len(grp) else 0
+            cost += CALL + 1e-3 * w * len(grp)
+            groups.append((w, grp, per))
+        cost += max(off, on)
+        if best is None or cost < best[0]:
+            best = (cost, groups)
+    calls = []
+    for w, grp, per in sorted(best[1], key=lambda g: (not any(d in far for d in g[1]), -g[0])):
+        used, tr = set(), {}
+        for d in sorted(grp, key=lambda d: (d not in far, d)):
+            free = [b for b in bits(masks[d]) if b not in used and (d in far or b not in pool)][:per]
+            used.update(free)
+            tr[d] = (min(wins[d][0], hi - w), free)
+        calls.append((w, tr))
+    return calls
+
+
+def relay_cores(n, cores, host, win, over, topo):
+    pairs = []
+    for j in range(n):
+        dst = [cores[e] for e in over[j]]
+        by = {}
+        for c in range(WORLD):
+            if (topo.host(c) == topo.host(dst[0]) and topo.same_plane(cores[j], c) and topo.die(c) != topo.die(cores[j])
+                    and all(topo.may_write(c, d) for d in dst)):
+                by.setdefault((topo.host(c), topo.chip(c)), []).append(c)
+        for h, cs in by.items():
+            home = sum(win[j][e][1] - win[j][e][0] for e in over[j] if (host[e], topo.chip(cores[e])) == h)
+            if len(cs) >= 2:
+                pairs.append((-home, h, j, cs[:2]))
+    relay, taken = {}, set()
+    for home, h, j, cs in sorted(pairs):
+        if j not in relay and h not in taken:
+            relay[j] = cs
+            taken.add(h)
+    return relay
 
 
 def plan(T, topo):
+    if CACHE:
+        return CACHE
+    P = CACHE
     cnt, cores = T.tables["CNT"], T.cores
     n = len(cores)
     host = [topo.host(c) for c in cores]
-    f0 = min(e for e in range(n) if host[e] != host[0]) - (K - 1)
-    seq = [(f0 + i) % n for i in range(n + K - 1)]
-    at = {e: next(i for i in range(n) if seq[i:i + K] == [(e - K + 1 + k) % n for k in range(K)]) for e in range(n)}
-    P = {"n": n, "f0": f0, "seq": seq, "at": at, "host": host}
-    pos = [[sum(cnt[j][f] for f in seq[:i]) for i in range(len(seq) + 1)] for j in range(n)]
-    P["pos"] = pos
-    win = [[(pos[j][at[e]], pos[j][at[e] + K]) for e in range(n)] for j in range(n)]
-    P["win"] = win
+    rank = {c: i for i, c in enumerate(cores)}
+    P["head"], P["win"] = [], []
+    for j in range(n):
+        f0 = (min(e for e in range(n) if host[e] != host[j]) - K + 1) % n
+        pos = [sum(cnt[j][(f0 + i) % n] for i in range(m)) for m in range(2 * n + 1)]
+        at = [(e - K + 1 - f0) % n for e in range(n)]
+        P["head"].append(sum(cnt[j][:f0]) % NC)
+        P["win"].append([(pos[i], pos[i + K]) for i in at])
+    win = P["win"]
     live = lambda j, e: j != e and win[j][e][1] > win[j][e][0]
-    P["inside"] = [[e for e in range(n) if host[e] == host[j] and live(j, e)] for j in range(n)]
-    P["across"] = [[e for e in range(n) if host[e] != host[j] and live(j, e)] for j in range(n)]
-    P["run"] = [(min(win[j][e][0] for e in P["across"][j]), max(win[j][e][1] for e in P["across"][j])) for j in range(n)]
-    width = {}
-    for kind in ("inside", "across"):
-        w = [max(win[j][e][1] - win[j][e][0] for e in P[kind][j]) for j in range(n)]
-        while True:
-            short = [[j for j in range(n) if e in P[kind][j]] for e in range(n)
-                     if sum(w[j] for j in range(n) if e in P[kind][j]) < NC]
-            if not short:
-                break
-            w[min(short[0], key=lambda j: w[j])] += 4
-        width[kind] = w
-    P["width"] = width
-    P["slot"] = {}
-    for kind in ("inside", "across"):
-        for e in range(n):
-            o, s = 0, {}
-            for j in range(n):
-                if e in P[kind][j]:
-                    s[j] = o
-                    o += width[kind][j]
-            P["slot"][kind, e] = (s, o)
-    start = {}
+    near = [[e for e in range(n) if host[e] == host[j] and live(j, e)] for j in range(n)]
+    over = [[e for e in range(n) if host[e] != host[j] and live(j, e)] for j in range(n)]
+    wide = {}
+    for e in range(n):
+        js = [j for j in range(n) if e in near[j]]
+        short = NC - sum(win[j][e][1] - win[j][e][0] for j in js)
+        thin = min(js, key=lambda j: win[j][e][1] - win[j][e][0])
+        for j in js:
+            s, t = win[j][e]
+            m = short if j == thin and short > 0 else 0
+            wide[j, e] = (s - m, t) if s >= m else (s, t + m)
+    calls = P["calls"] = {}
+    slots = P["slots"] = {(e, k): [] for e in range(n) for k in "bc"}
+
+    def put(core, wait, bufs, tr):
+        calls.setdefault(core, []).append((wait, bufs, tr))
+
+    def windows(kind, j, groups):
+        out = []
+        for w, tr in groups:
+            r = []
+            for d, (a, m) in tr.items():
+                s = {"j": j, "a": a, "w": w, "inc": 0}
+                slots[rank[d], kind].append(s)
+                r.append((d, m, a, s))
+            out.append((w, r))
+        return out
+
+    def send(core, wait, bufs, base, wins):
+        for w, tr in wins:
+            put(core, wait, bufs, [(d, m, a - base, s, w) for d, m, a, s in tr])
+            for d, m, a, s in tr:
+                s["inc"] += len(m)
+
+    relay = relay_cores(n, cores, host, win, over, topo)
     for j in range(n):
-        for e in P["inside"][j]:
-            start[j, e] = min(win[j][e][0], pos[j][-1] - width["inside"][j])
-        for e in P["across"][j]:
-            start[j, e] = min(win[j][e][0], P["run"][j][1] - width["across"][j])
-    P["start"] = start
-    taken, relay = set(), []
-    for j in range(n):
-        src = cores[j]
-        dst = [cores[e] for e in P["across"][j]]
-        by = {}
-        for c in range(WORLD):
-            if (topo.host(c) == topo.host(dst[0]) and topo.same_plane(src, c) and topo.die(c) != topo.die(src)
-                    and all(topo.may_write(c, d) for d in dst)):
-                by.setdefault(topo.chip(c), []).append(c)
-        ranked = [topo.chip(d) for d in dst]
-        chip = min((h for h in by if (topo.host(dst[0]), h) not in taken and len(by[h]) >= 2), key=lambda h: (h not in ranked, h))
-        taken.add((topo.host(dst[0]), chip))
-        relay.append(by[chip][:2])
-    P["relay"] = relay
-    arr = {}
-    for j in range(n):
-        for kind, srcs, sem in (("inside", [cores[j]] * 2, "bin"), ("across", relay[j], "cin")):
-            for s in srcs:
-                for d, m in share(s, [cores[e] for e in P[kind][j]], topo).items():
-                    arr[d, sem] = arr.get((d, sem), 0) + len(bits(m))
-    P["arr"] = arr
+        me = cores[j]
+        a, b = min(win[j][e][0] for e in over[j]), max(win[j][e][1] for e in over[j])
+        m = bits(topo.mask(me, relay[j][0]))
+        cw = windows("c", j, pack(relay[j][0], {cores[e]: win[j][e] for e in over[j]}, b, topo))
+        bw = windows("b", j, pack(me, {cores[e]: wide[j, e] for e in near[j]}, 2 * NC, topo))
+        helper = next(c for c in range(WORLD) if c != me and topo.host(c) == host[j] and topo.chip(c) == topo.chip(me)
+                      and topo.die(c) == topo.die(me) and all(topo.may_write(c, cores[e]) for e in near[j]))
+        hm = [x for x in bits(topo.mask(me, helper)) if x not in m][:len(m)]
+        lo, hi = min(a for w, tr in bw for d, x, a, s in tr), max(a + w for w, tr in bw for d, x, a, s in tr)
+        w = max(b - a, hi - lo)
+        lo = min(lo, 2 * NC - w)
+        put(me, ("qx", 1), ("xq", "rq"), [(relay[j][0], m, a, "ra", b - a)])
+        put(me, ("qy", 1), ("xs", "rs"), [(relay[j][1], m, a, "ra", w), (helper, hm, lo, "ra", w)])
+        send(me, ("qy", 1), ("xq", "bq"), 0, bw)
+        send(helper, ("ra", len(hm)), ("rs", "bs"), lo, bw)
+        send(relay[j][0], ("ra", len(m)), ("rq", "cq"), a, cw)
+        send(relay[j][1], ("ra", len(m)), ("rs", "cs"), a, cw)
+    P["banks"], P["arr"] = {}, {}
+    for (e, kind), sl in slots.items():
+        sl.sort(key=lambda s: s["j"])
+        o = 0
+        for s in sl:
+            s["o"] = o
+            o += s["w"]
+        load = [sum(max(64, cnt[s["j"]][(e - k) % n]) + 50 for k in range(K) if cnt[s["j"]][(e - k) % n]) for s in sl]
+        cut = min(range(1, len(sl)), key=lambda c: max(sum(load[:c]), sum(load[c:])))
+        for i, s in enumerate(sl):
+            s["sem"] = "%s%d" % (kind, i >= cut)
+            P["arr"][e, s["sem"]] = P["arr"].get((e, s["sem"]), 0) + s["inc"]
+        P["banks"][e, kind] = []
+        for part in (sl[:cut], sl[cut:]):
+            lo = min(part[0]["o"], o - NC)
+            hi = max(part[-1]["o"] + part[-1]["w"], lo + NC)
+            need = sorted({s["sem"] for s in sl if s["o"] < hi and s["o"] + s["w"] > lo})
+            P["banks"][e, kind].append((part, lo, hi, need))
     return P
 
 
-def send_windows(g, T, topo, core, P, j, kind, codes, base, sem):
-    src, dst = {("inside", True): ("xq", "bq"), ("inside", False): ("xs", "bs"),
-                ("across", True): ("rq", "cq"), ("across", False): ("rs", "cs")}[kind, codes]
-    w = P["width"][kind][j]
-    masks = share(core, [T.cores[e] for e in P[kind][j]], topo)
-    tr = []
-    for e in P[kind][j]:
-        d = T.cores[e]
-        rid, pid = topo.addr(d, core)
-        a, o = P["start"][j, e] - base, P["slot"][kind, e][0][j]
-        s, t = T[src][:, a:a + w], T[dst][:, o:o + w]
-        if codes:
-            s, t = s.bitcast(dt.uint8), t.bitcast(dt.uint8)
-        tr.append(RemoteDMATransfer(dst_ids=[DstId(rid=rid, pnc=pid)], dma_engine_mask=masks[d], remote_sem=T.sem[sem], src=s, dst=t))
-    g.remote_dma_fused(tr, local_sem=T.sem.sent)
-    return sum(len(bits(m)) for m in masks.values())
-
-
-def relay_program(g, core, T, topo, P):
-    for j in range(P["n"]):
-        if core in P["relay"][j]:
-            g.wait_ge(T.sem.ra, len(bits(topo.mask(T.cores[j], core))))
-            g.wait_ge(T.sem.sent, send_windows(g, T, topo, core, P, j, "across", core == P["relay"][j][0], P["run"][j][0], "cin"))
-
-
-def bank_views(slots, total, cost):
-    js = sorted(slots)
-    cut = min(range(1, len(js)), key=lambda c: max(sum(cost[j] for j in js[:c]), sum(cost[j] for j in js[c:])))
-    mid = slots[js[cut]]
-    return [(js[:cut], 0, max(mid, NC)), (js[cut:], min(mid, total - NC), total)]
+def remote_calls(g, T, topo, core, P):
+    sent, last = 0, None
+    for wait, (src, dst), tr in P["calls"].get(core, []):
+        if wait != last:
+            g.wait_ge(T.sem[wait[0]], wait[1])
+            last = wait
+        ts = []
+        for d, m, a, s, w in tr:
+            rid, pid = topo.addr(d, core)
+            o, sem = (s["o"], s["sem"]) if isinstance(s, dict) else (0, s)
+            f, t = T[src][:, a:a + w], T[dst][:, o:o + w]
+            if src in ("xq", "rq"):
+                f, t = f.bitcast(dt.uint8), t.bitcast(dt.uint8)
+            ts.append(RemoteDMATransfer(dst_ids=[DstId(rid=rid, pnc=pid)], dma_engine_mask=sum(m), remote_sem=T.sem[sem], src=f, dst=t))
+            sent += len(m)
+        g.remote_dma_fused(ts, local_sem=T.sem.sent)
+    if sent:
+        g.wait_ge(T.sem.sent, sent)
 
 
 def rank_program(g, core, T, topo):
-    rank = T.rank_of(core)
+    e = T.rank_of(core)
     P = plan(T, topo)
-    if rank is None:
-        relay_program(g, core, T, topo, P)
+    if e is None:
+        remote_calls(g, T, topo, core, P)
         return
-    cnt, n, win = T.tables["CNT"], P["n"], P["win"]
-    pos = P["pos"][rank]
-    tail = pos[n - P["f0"]]
-    ext = pos[-1]
-    g.sync.dma_start(T.xt[:, 0:4 * tail], T.x[:, 4 * (NC - tail):4 * NC]).then_inc(T.sem.ldx, 16)
-    g.scalar.dma_start(T.xt[:, 4 * tail:4 * ext], T.x[:, 0:4 * (ext - tail)]).then_inc(T.sem.ldx, 16)
-    g.sync.dma_start(T.wt[:], T.w[:]).then_inc(T.sem.ldw, 16)
-    g.vector.wait_ge(T.sem.ldx, 32)
-    g.vector.quantize_mx(T.xq[:, 0:ext], T.xs[:, 0:ext], T.xt[:, 0:4 * ext]).then_inc(T.sem.qx, 1)
+    cnt, win, cores = T.tables["CNT"], P["win"], T.cores
+    n = len(cores)
+    head = P["head"][e]
+    g.sync.dma_start(T.xt[:, 0:4 * (NC - head)], T.x[:, 4 * head:4 * NC]).then_inc(T.sem.ldx, 16)
+    if head:
+        g.scalar.dma_start(T.xt[:, 4 * (NC - head):4 * NC], T.x[:, 0:4 * head]).then_inc(T.sem.ldx, 16)
+    g.scalar.dma_start(T.wt[:], T.w[:]).then_inc(T.sem.ldw, 16)
+    g.vector.wait_ge(T.sem.ldx, 32 if head else 16)
+    g.vector.quantize_mx(T.xq[:, 0:NC], T.xs[:, 0:NC], T.xt[:]).then_inc(T.sem.qx, 1)
+    g.vector.quantize_mx(T.xq[:, NC:2 * NC], T.xs[:, NC:2 * NC], T.xt[:]).then_inc(T.sem.qy, 1)
     g.vector.wait_ge(T.sem.ldw, 16)
     g.vector.quantize_mx(T.wq[:], T.ws[:], T.wt[:]).then_inc(T.sem.qw, 1)
-    g.wait_ge(T.sem.qx, 1)
-    sent = 0
-    a, b = P["run"][rank]
-    for to, codes in zip(P["relay"][rank], (True, False)):
-        rid, pid = topo.addr(to, core)
-        m = topo.mask(core, to)
-        if codes:
-            g.remote_dma(T.rq[:, 0:b - a].bitcast(dt.uint8), T.xq[:, a:b].bitcast(dt.uint8), T.sem.ra, T.sem.sent, pid, rid, m)
-        else:
-            g.remote_dma(T.rs[:, 0:b - a], T.xs[:, a:b], T.sem.ra, T.sem.sent, pid, rid, m)
-        sent += len(bits(m))
-    for codes in (True, False):
-        sent += send_windows(g, T, topo, core, P, rank, "inside", codes, 0, "bin")
-    g.wait_ge(T.sem.sent, sent)
-    e = rank
-    a = min(win[e][e][0], ext - NC)
-    groups = [(T.p0, T.sem.m0, "own", [e], T.xq, T.xs, a, a + NC)]
-    cost = {j: sum(max(64, cnt[j][(e - k) % n]) + 40 for k in range(K) if cnt[j][(e - k) % n]) for j in range(n)}
-    for kind, q, s, banks in (("inside", T.bq, T.bs, (1, 2)), ("across", T.cq, T.cs, (3, 4))):
-        slots, total = P["slot"][kind, e]
-        for i, (js, lo, hi) in zip(banks, bank_views(slots, total, cost)):
-            groups.append((T["p%d" % i], T.sem["m%d" % i], kind, js, q, s, lo, hi))
+    remote_calls(g, T, topo, core, P)
+    own = min(win[e][e][0], NC)
+    groups = [("p0", "m0", T.xq, T.xs, [{"j": e, "a": own, "o": own, "w": NC}], own, own + NC, [])]
+    for kind, q, s, i in (("b", T.bq, T.bs, 1), ("c", T.cq, T.cs, 3)):
+        for b, (sl, lo, hi, need) in enumerate(P["banks"][e, kind]):
+            groups.append(("p%d" % (i + b), "m%d" % (i + b), q, s, sl, lo, hi, need))
     g.tensor.wait_ge(T.sem.qx, 1)
+    g.tensor.wait_ge(T.sem.qy, 1)
     g.tensor.wait_ge(T.sem.qw, 1)
-    for i, (bank, sem, kind, js, q, s, lo, hi) in enumerate(groups):
-        if i == 1:
-            g.tensor.wait_ge(T.sem.bin, P["arr"][core, "bin"])
-        if i == 3:
-            g.tensor.wait_ge(T.sem.cin, P["arr"][core, "cin"])
-        g.tensor.matmul_mx(bank[:, 0:hi - lo], T.wq[:], T.ws[:], q[:, lo:hi], s[:, lo:hi], True, True).then_inc(sem, 1)
-    done = {"lo": 0, "hi": 0}
-    for i, (bank, sem, kind, js, q, s, lo, hi) in enumerate(groups):
+    seen = set()
+    for bank, sem, q, s, sl, lo, hi, need in groups:
+        for x in need:
+            if x not in seen:
+                g.tensor.wait_ge(T.sem[x], P["arr"][e, x])
+                seen.add(x)
+        g.tensor.matmul_mx(T[bank][:, 0:hi - lo], T.wq[:], T.ws[:], q[:, lo:hi], s[:, lo:hi], True, True).then_inc(T.sem[sem], 1)
+    done = {}
+    for i, (bank, sem, q, s, sl, lo, hi, need) in enumerate(groups):
         on_scalar = i in (2, 4)
-        (g.scalar if on_scalar else g.vector).wait_ge(sem, 1)
+        (g.scalar if on_scalar else g.vector).wait_ge(T.sem[sem], 1)
         for k in range(K):
             f = (e - k) % n
-            for j in js:
-                c = cnt[j][f]
+            for x in sl:
+                j, c = x["j"], cnt[x["j"]][f]
                 if not c:
                     continue
-                o = win[j][e][0] + sum(cnt[j][(e - m) % n] for m in range(k + 1, K))
-                if kind != "own":
-                    o += P["slot"][kind, e][0][j] - P["start"][j, e]
-                o -= lo
+                o = win[j][e][0] + sum(cnt[j][(e - m) % n] for m in range(k + 1, K)) - x["a"] + x["o"] - lo
                 to = k * NC + sum(cnt[i2][f] for i2 in range(j))
-                half = "lo" if k < 2 else "hi"
-                done[half] += 1
+                part = "early" if i < 3 else "f%d" % k
+                done[part] = done.get(part, 0) + 1
                 if on_scalar:
-                    g.scalar.activation(T.ys[:, to:to + c], bank[:, o:o + c], ActivationFunctionType.Copy).then_inc(T.sem[half], 1)
+                    g.scalar.activation(T.ys[:, to:to + c], T[bank][:, o:o + c], ActivationFunctionType.Copy).then_inc(T.sem[part], 1)
                 else:
-                    g.vector.tensor_copy(T.ys[:, to:to + c], bank[:, o:o + c]).then_inc(T.sem[half], 1)
-    g.sync.wait_ge(T.sem.lo, done["lo"])
-    g.sync.dma_start(T.y[:, 0:2 * NC], T.ys[:, 0:2 * NC]).then_inc(T.sem.st, 16)
-    g.scalar.wait_ge(T.sem.hi, done["hi"])
-    g.scalar.dma_start(T.y[:, 2 * NC:4 * NC], T.ys[:, 2 * NC:4 * NC]).then_inc(T.sem.st, 16)
-    g.sync.wait_ge(T.sem.st, 32)
+                    g.vector.tensor_copy(T.ys[:, to:to + c], T[bank][:, o:o + c]).then_inc(T.sem[part], 1)
+    st = 0
+    for part in (True, False):
+        js = [j for j in range(n) if (topo.host(cores[j]) == topo.host(core)) == part]
+        for k in range(K):
+            f = (e - k) % n
+            lo = k * NC + sum(cnt[j][f] for j in range(js[0]))
+            hi = lo + sum(cnt[j][f] for j in js)
+            if hi == lo:
+                continue
+            if part and not st:
+                g.sync.wait_ge(T.sem.early, done["early"])
+            if not part:
+                g.sync.wait_ge(T.sem["f%d" % k], done["f%d" % k])
+            g.sync.dma_start(T.y[:, lo:hi], T.ys[:, lo:hi]).then_inc(T.sem.st, 16)
+            st += 16
+    g.sync.wait_ge(T.sem.st, st)

@@ -1,30 +1,28 @@
 from concourse.bass import DstId, RemoteDMATransfer
 from concourse.mybir import dt, ActivationFunctionType
 
+BANKS = 8
 SCRATCH = {
     "xt": ("sbuf", [128, 512], "bfloat16"),
     "wt": ("sbuf", [128, 512], "bfloat16"),
-    "xq": ("sbuf", [128, 256], "float8_e4m3fn_x4"),
-    "xs": ("sbuf", [128, 256], "uint8"),
+    "xq": ("sbuf", [128, 1024], "float8_e4m3fn_x4"),
+    "xs": ("sbuf", [128, 1024], "uint8"),
     "wq": ("sbuf", [128, 128], "float8_e4m3fn_x4"),
     "ws": ("sbuf", [128, 128], "uint8"),
     "rq": ("sbuf", [128, 256], "float8_e4m3fn_x4"),
     "rs": ("sbuf", [128, 256], "uint8"),
-    "bq": ("sbuf", [128, 640], "float8_e4m3fn_x4"),
-    "bs": ("sbuf", [128, 640], "uint8"),
-    "cq": ("sbuf", [128, 640], "float8_e4m3fn_x4"),
-    "cs": ("sbuf", [128, 640], "uint8"),
     "ys": ("sbuf", [128, 512], "float32"),
-    "p0": ("psum", [128, 512], "float32"),
-    "p1": ("psum", [128, 512], "float32"),
-    "p2": ("psum", [128, 512], "float32"),
-    "p3": ("psum", [128, 512], "float32"),
-    "p4": ("psum", [128, 512], "float32"),
 }
-SEMAPHORES = ["ldx", "ldw", "qx", "qy", "qw", "sent", "ra", "b0", "b1", "c0", "c1", "m0", "m1", "m2", "m3", "m4",
-              "early", "f0", "f1", "f2", "f3", "st"]
+for _i in range(BANKS):
+    SCRATCH["p%d" % _i] = ("psum", [128, 512], "float32")
+SEMAPHORES = (["ldx", "ldw", "qx", "qy", "qw", "sent", "ra", "st"] + ["a%d" % i for i in range(8)] + ["m%d" % i for i in range(9)]
+              + ["t%d" % i for i in range(12)] + ["e%d" % i for i in range(4)])
 K, NC, WORLD = 4, 128, 256
+BUDGET = 357632
 CALL, ROW, BYTE = 0.1, 0.012, 1 / 14000.
+ROWC, GAIN, LAG = 0.02, 0.1, 0.3
+HOP = 1.0
+THIN, THIN0 = 40, 24
 CACHE = {}
 
 
@@ -46,28 +44,25 @@ def pack(core, wins, hi, topo):
     masks = {d: topo.mask(core, d) for d in wins}
     few = min(len(bits(m)) for m in masks.values())
     far = [d for d in wins if len(bits(masks[d])) == few]
+    alone = [[d] for d in wins if d not in far]
     pool = bits(masks[far[0]])
     best = None
-    for part in partitions(sorted(wins)):
-        cost, off, on, groups = 0, 0, 0, []
+    for part in partitions(sorted(far)):
+        cost, groups = 0, []
         for grp in part:
             w = max(wins[d][1] - wins[d][0] for d in grp)
-            out = sum(1 for d in grp if d in far)
             per = 1
-            while 2 * per * max(1, out) <= len(pool):
+            while 2 * per * len(grp) <= len(pool):
                 per *= 2
-            t = NC / per * (ROW + 4 * w * BYTE)
-            off += t if out else 0
-            on += t if out < len(grp) else 0
-            cost += CALL + 1e-3 * w * len(grp)
+            cost += CALL + 1e-3 * w * len(grp) + NC / per * (ROW + 4 * w * BYTE)
             groups.append((w, grp, per))
-        cost += max(off, on)
         if best is None or cost < best[0]:
             best = (cost, groups)
+    groups = sorted(best[1], key=lambda g: -g[0]) + [(wins[d][1] - wins[d][0], [d], len(pool)) for [d] in alone]
     calls = []
-    for w, grp, per in sorted(best[1], key=lambda g: (not any(d in far for d in g[1]), -g[0])):
+    for w, grp, per in groups:
         used, tr = set(), {}
-        for d in sorted(grp, key=lambda d: (d not in far, d)):
+        for d in sorted(grp):
             free = [b for b in bits(masks[d]) if b not in used and (d in far or b not in pool)][:per]
             used.update(free)
             tr[d] = (min(wins[d][0], hi - w), free)
@@ -96,6 +91,37 @@ def relay_cores(n, cores, host, win, over, topo):
     return relay
 
 
+def share(slots, local, a, b, most):
+    cost = lambda w: NC / 8 * (ROWC + 4 * w * BYTE)
+    best = (cost(b - a) + sum(cost(s["w"]) for s in slots if s is not local) - GAIN, None)
+    for low in (True, False):
+        for p in range(a + 4, b, 4):
+            for q in range(p, min(b, p + most + 1), 4):
+                one, two = ((p, b), (a, q)) if low else ((a, q), (p, b))
+                px, py = [], []
+                for s in slots:
+                    lo, hi = s["a"], s["a"] + s["w"]
+                    if one[0] <= lo and hi <= one[1]:
+                        px.append((s, lo, hi))
+                    elif two[0] <= lo and hi <= two[1]:
+                        py.append((s, lo, hi))
+                    elif low:
+                        px.append((s, q, hi))
+                        py.append((s, lo, q))
+                    else:
+                        px.append((s, lo, p))
+                        py.append((s, p, hi))
+                if any(y <= x for s, x, y in px + py):
+                    continue
+                t1 = cost(one[1] - one[0])
+                t2 = t1 + cost((b - a) / 4) + cost(two[1] - two[0]) + sum(cost(y - x) for s, x, y in py)
+                t1 += sum(cost(y - x) for s, x, y in px if s is not local)
+                v = max(t1, t2 - LAG) + .1 * t2 + .002 * (q - p)
+                if v < best[0]:
+                    best = (v, (one, two, px, py, q - p))
+    return best[1]
+
+
 def plan(T, topo):
     if CACHE:
         return CACHE
@@ -104,100 +130,129 @@ def plan(T, topo):
     n = len(cores)
     host = [topo.host(c) for c in cores]
     rank = {c: i for i, c in enumerate(cores)}
+    spot = lambda c: (topo.host(c), topo.chip(c))
     P["head"], P["win"] = [], []
     for j in range(n):
-        f0 = (min(e for e in range(n) if host[e] != host[j]) - K + 1) % n
+        other = [e for e in range(n) if host[e] != host[j]]
+        mine = [e for e in range(n) if host[e] == host[j]]
+        f0 = (min(other) - K + 1) % n
+        if max((e - K + 1) % n + K for e in other) <= n:
+            f0 = 0
         pos = [sum(cnt[j][(f0 + i) % n] for i in range(m)) for m in range(2 * n + 1)]
-        at = [(e - K + 1 - f0) % n for e in range(n)]
+        at = {e: (e - K + 1 - f0) % n for e in range(n)}
+        tries = []
+        for c in range(n - K + 2):
+            b = {e: at[e] + n if at[e] < c else at[e] for e in mine}
+            tries.append((max(b.values()) - min(b.values()), c, b))
+        at.update(min(tries, key=lambda x: x[:2])[2])
         P["head"].append(sum(cnt[j][:f0]) % NC)
-        P["win"].append([(pos[i], pos[i + K]) for i in at])
+        P["win"].append([(pos[at[e]], pos[at[e] + K]) for e in range(n)])
     win = P["win"]
     live = lambda j, e: j != e and win[j][e][1] > win[j][e][0]
     near = [[e for e in range(n) if host[e] == host[j] and live(j, e)] for j in range(n)]
     over = [[e for e in range(n) if host[e] != host[j] and live(j, e)] for j in range(n)]
-    wide = {}
-    for e in range(n):
-        js = [j for j in range(n) if e in near[j]]
-        short = NC - sum(win[j][e][1] - win[j][e][0] for j in js)
-        thin = min(js, key=lambda j: win[j][e][1] - win[j][e][0])
-        for j in js:
-            s, t = win[j][e]
-            m = short if j == thin and short > 0 else 0
-            wide[j, e] = (s - m, t) if s >= m else (s, t + m)
     calls = P["calls"] = {}
-    slots = P["slots"] = {(e, k): [] for e in range(n) for k in "bc"}
-
-    def put(core, wait, bufs, tr):
-        calls.setdefault(core, []).append((wait, bufs, tr))
+    slots = P["slots"] = {e: [] for e in range(n)}
 
     def windows(kind, j, groups):
         out = []
         for w, tr in groups:
             r = []
             for d, (a, m) in tr.items():
-                s = {"j": j, "a": a, "w": w, "inc": 0}
-                slots[rank[d], kind].append(s)
+                s = {"j": j, "a": a, "w": w, "inc": 0, "kind": kind, "t": 0, "to": d}
+                slots[rank[d]].append(s)
                 r.append((d, m, a, s))
             out.append((w, r))
         return out
 
-    def send(core, wait, bufs, base, wins):
+    def pieces(core, px, pool):
+        by = {}
+        for s, x, y in px:
+            by.setdefault((spot(s["to"]) == spot(core), x - y), []).append((s["to"], x, s))
+        out = []
+        for (on, w), ds in sorted(by.items(), key=lambda z: z[0]):
+            per = len(pool)
+            while per * len(ds) > len(pool):
+                per //= 2
+            es = [e for e in bits(topo.mask(core, ds[0][0])) if e not in pool] if on else pool
+            out.append((-w, [(d, es[i * per:(i + 1) * per], x, s) for i, (d, x, s) in enumerate(ds)]))
+        return out
+
+    def send(core, wait, bufs, base, wins, t):
+        free = {}
         for w, tr in wins:
-            put(core, wait, bufs, [(d, m, a - base, s, w) for d, m, a, s in tr])
+            calls.setdefault(core, []).append((wait, bufs, base, [(d, m, a, s, w) for d, m, a, s in tr]))
+            t += CALL
             for d, m, a, s in tr:
-                s["inc"] += len(m)
+                end = max([t] + [free.get(x, 0) for x in m]) + NC / len(m) * (ROW + (4 if bufs[0][1] == "q" else 1) * w * BYTE)
+                for x in m:
+                    free[x] = end
+                if isinstance(s, dict):
+                    s["inc"] += len(m)
+                    s["t"] = max(s["t"], end)
+        return max(free.values())
 
     relay = relay_cores(n, cores, host, win, over, topo)
+    prep = {}
     for j in range(n):
         me = cores[j]
         a, b = min(win[j][e][0] for e in over[j]), max(win[j][e][1] for e in over[j])
         m = bits(topo.mask(me, relay[j][0]))
         cw = windows("c", j, pack(relay[j][0], {cores[e]: win[j][e] for e in over[j]}, b, topo))
-        bw = windows("b", j, pack(me, {cores[e]: wide[j, e] for e in near[j]}, 2 * NC, topo))
-        helper = next(c for c in range(WORLD) if c != me and topo.host(c) == host[j] and topo.chip(c) == topo.chip(me)
+        bw = windows("b", j, pack(me, {cores[e]: win[j][e] for e in near[j]}, 2 * NC, topo))
+        helper = next(c for c in range(WORLD) if c != me and spot(c) == spot(me)
                       and topo.die(c) == topo.die(me) and all(topo.may_write(c, cores[e]) for e in near[j]))
         hm = [x for x in bits(topo.mask(me, helper)) if x not in m][:len(m)]
         lo, hi = min(a for w, tr in bw for d, x, a, s in tr), max(a + w for w, tr in bw for d, x, a, s in tr)
         w = max(b - a, hi - lo)
-        lo = min(lo, 2 * NC - w)
-        put(me, ("qx", 1), ("xq", "rq"), [(relay[j][0], m, a, "ra", b - a)])
-        put(me, ("qy", 1), ("xs", "rs"), [(relay[j][1], m, a, "ra", w), (helper, hm, lo, "ra", w)])
-        send(me, ("qy", 1), ("xq", "bq"), 0, bw)
-        send(helper, ("ra", len(hm)), ("rs", "bs"), lo, bw)
-        send(relay[j][0], ("ra", len(m)), ("rq", "cq"), a, cw)
-        send(relay[j][1], ("ra", len(m)), ("rs", "cs"), a, cw)
-    P["banks"], P["arr"] = {}, {}
-    for (e, kind), sl in slots.items():
-        sl.sort(key=lambda s: s["j"])
-        o = 0
-        for s in sl:
-            s["o"] = o
-            o += s["w"]
-        load = [sum(max(64, cnt[s["j"]][(e - k) % n]) + 50 for k in range(K) if cnt[s["j"]][(e - k) % n]) for s in sl]
-        cut = min(range(1, len(sl)), key=lambda c: max(sum(load[:c]), sum(load[c:])))
+        prep[j] = (a, b, m, cw, bw, helper, hm, min(lo, 2 * NC - w), w)
+    spare = {h: BUDGET - sum(4 * NC * (p[1] - p[0]) + NC * p[-1] for j, p in prep.items() if host[j] != h) for h in set(host)}
+    used = set(spot(c) for c in cores) | set(spot(c) for r in relay.values() for c in r)
+    load = lambda j: sum(win[j][e][1] - win[j][e][0] for e in over[j]) - max(win[j][e][1] - win[j][e][0] for e in over[j])
+    for j in sorted(range(n), key=lambda j: -load(j)):
+        me = cores[j]
+        a, b, m, cw, bw, helper, hm, lo, w = prep[j]
+        h = topo.host(relay[j][0])
+        sl = [s for x, tr in cw for d, y, c, s in tr]
+        local = next((s for s in sl if spot(s["to"]) == spot(relay[j][0])), None)
+        two = share(sl, local, a, b, max(0, spare[h] // (4 * NC)))
+        a1, b1, first = a, b, cw
+        if two:
+            (a1, b1), (a2, b2), px, py, both = two
+            spare[h] -= 4 * NC * both
+            third = next(c for c in range(WORLD) if topo.host(c) == h and spot(c) not in used and topo.same_plane(me, c)
+                         and topo.die(c) == topo.die(me) and all(topo.may_write(c, s["to"]) for s in sl))
+            used.add(spot(third))
+            first = pieces(relay[j][0], px, m)
+        t = send(me, ("qx" if b <= NC else "qy", 1), ("xq", "rq"), 0, [(b1 - a1, [(relay[j][0], m, a1, "ra")])], 0)
+        u = v = send(me, ("qy", 1), ("xs", "rs"), 0, [(w, [(relay[j][1], m, a, "ra"), (helper, hm, lo, "ra")])], t)
+        if two:
+            v = send(me, ("qy", 1), ("xq", "rq"), 0, [(b2 - a2, [(third, m, a2, "ra")])], u)
+            send(third, ("ra", len(m)), ("rq", "xq"), a2, pieces(third, py, m), v + HOP)
+        send(me, ("qy", 1), ("xq", "xq"), 0, bw, v)
+        send(helper, ("ra", len(hm)), ("rs", "xs"), lo, bw, u + HOP)
+        send(relay[j][0], ("ra", len(m)), ("rq", "xq"), a1, first, t + HOP)
+        send(relay[j][1], ("ra", len(m)), ("rs", "xs"), a, cw, u + HOP)
+    for e, sl in slots.items():
+        sl.sort(key=lambda s: (s["kind"], s["t"]))
+        o = 2 * NC
         for i, s in enumerate(sl):
-            s["sem"] = "%s%d" % (kind, i >= cut)
-            P["arr"][e, s["sem"]] = P["arr"].get((e, s["sem"]), 0) + s["inc"]
-        P["banks"][e, kind] = []
-        for part in (sl[:cut], sl[cut:]):
-            lo = min(part[0]["o"], o - NC)
-            hi = max(part[-1]["o"] + part[-1]["w"], lo + NC)
-            need = sorted({s["sem"] for s in sl if s["o"] < hi and s["o"] + s["w"] > lo})
-            P["banks"][e, kind].append((part, lo, hi, need))
+            s["o"], s["sem"] = o, "a%d" % i
+            o += s["w"]
     return P
 
 
 def remote_calls(g, T, topo, core, P):
     sent, last = 0, None
-    for wait, (src, dst), tr in P["calls"].get(core, []):
+    for wait, (src, dst), base, tr in P["calls"].get(core, []):
         if wait != last:
             g.wait_ge(T.sem[wait[0]], wait[1])
             last = wait
         ts = []
         for d, m, a, s, w in tr:
             rid, pid = topo.addr(d, core)
-            o, sem = (s["o"], s["sem"]) if isinstance(s, dict) else (0, s)
-            f, t = T[src][:, a:a + w], T[dst][:, o:o + w]
+            o, sem = (s["o"] + a - s["a"], s["sem"]) if isinstance(s, dict) else (0, s)
+            f, t = T[src][:, a - base:a - base + w], T[dst][:, o:o + w]
             if src in ("xq", "rq"):
                 f, t = f.bitcast(dt.uint8), t.bitcast(dt.uint8)
             ts.append(RemoteDMATransfer(dst_ids=[DstId(rid=rid, pnc=pid)], dma_engine_mask=sum(m), remote_sem=T.sem[sem], src=f, dst=t))
@@ -213,65 +268,83 @@ def rank_program(g, core, T, topo):
     if e is None:
         remote_calls(g, T, topo, core, P)
         return
-    cnt, win, cores = T.tables["CNT"], P["win"], T.cores
-    n = len(cores)
+    cnt, win = T.tables["CNT"], P["win"]
+    n = len(T.cores)
     head = P["head"][e]
     g.sync.dma_start(T.xt[:, 0:4 * (NC - head)], T.x[:, 4 * head:4 * NC]).then_inc(T.sem.ldx, 16)
     if head:
         g.scalar.dma_start(T.xt[:, 4 * (NC - head):4 * NC], T.x[:, 0:4 * head]).then_inc(T.sem.ldx, 16)
-    g.scalar.dma_start(T.wt[:], T.w[:]).then_inc(T.sem.ldw, 16)
-    g.vector.wait_ge(T.sem.ldx, 32 if head else 16)
+    loaded = 32 if head else 16
+    g.sync.wait_ge(T.sem.ldx, loaded)
+    g.sync.dma_start(T.wt[:], T.w[:]).then_inc(T.sem.ldw, 16)
+    g.vector.wait_ge(T.sem.ldx, loaded)
     g.vector.quantize_mx(T.xq[:, 0:NC], T.xs[:, 0:NC], T.xt[:]).then_inc(T.sem.qx, 1)
     g.vector.quantize_mx(T.xq[:, NC:2 * NC], T.xs[:, NC:2 * NC], T.xt[:]).then_inc(T.sem.qy, 1)
     g.vector.wait_ge(T.sem.ldw, 16)
     g.vector.quantize_mx(T.wq[:], T.ws[:], T.wt[:]).then_inc(T.sem.qw, 1)
     remote_calls(g, T, topo, core, P)
+    sl = P["slots"][e]
+    when = {s["j"]: s["t"] for s in sl if s["kind"] == "c"}
+    late = sorted(when)
+    mine = [j for j in range(n) if j not in when]
+    beside = min(late) if min(late) > min(mine) else max(late)
+    cuts = []
+    for c in range(1, len(late)):
+        for ea in (late[:c], late[c:]):
+            cuts.append((max(when[j] for j in ea) + .1 * abs(len(ea) - len(late) / 2), ea))
+    first = min(cuts)[1]
+    stores, home, early = [], {}, {}
+    for k in range(K):
+        f = (e - k) % n
+        size = lambda js: sum(cnt[j][f] for j in js)
+        early[k] = sum(1 for j in mine if cnt[j][f])
+        part = {j: 1 if size(first) >= THIN and j in first else 2 for j in late}
+        part.update({j: 0 if size(mine) >= THIN0 else part[beside] for j in mine})
+        for ph in (0, 1, 2):
+            js = [j for j in range(n) if cnt[j][f] and part[j] == ph]
+            if js:
+                sem = "t%d" % len(stores)
+                for j in js:
+                    home[j, k] = sem if j in when else "e%d" % k
+                need = [("e%d" % k, early[k])] if any(j in mine for j in js) else []
+                if any(j in when for j in js):
+                    need.append((sem, sum(1 for j in js if j in when)))
+                lo = k * NC + sum(cnt[j][f] for j in range(js[0]))
+                stores.append((ph, k, lo, lo + size(js), need))
+    stores.sort(key=lambda s: s[:2])
     own = min(win[e][e][0], NC)
-    groups = [("p0", "m0", T.xq, T.xs, [{"j": e, "a": own, "o": own, "w": NC}], own, own + NC, [])]
-    for kind, q, s, i in (("b", T.bq, T.bs, 1), ("c", T.cq, T.cs, 3)):
-        for b, (sl, lo, hi, need) in enumerate(P["banks"][e, kind]):
-            groups.append(("p%d" % (i + b), "m%d" % (i + b), q, s, sl, lo, hi, need))
+    prods = [{"j": e, "a": own, "o": own, "w": NC}] + sl
     g.tensor.wait_ge(T.sem.qx, 1)
     g.tensor.wait_ge(T.sem.qy, 1)
     g.tensor.wait_ge(T.sem.qw, 1)
-    seen = set()
-    for bank, sem, q, s, sl, lo, hi, need in groups:
-        for x in need:
-            if x not in seen:
-                g.tensor.wait_ge(T.sem[x], P["arr"][e, x])
-                seen.add(x)
-        g.tensor.matmul_mx(T[bank][:, 0:hi - lo], T.wq[:], T.ws[:], q[:, lo:hi], s[:, lo:hi], True, True).then_inc(T.sem[sem], 1)
-    done = {}
-    for i, (bank, sem, q, s, sl, lo, hi, need) in enumerate(groups):
-        on_scalar = i in (2, 4)
-        (g.scalar if on_scalar else g.vector).wait_ge(T.sem[sem], 1)
+    for i, s in enumerate(prods):
+        if i:
+            g.tensor.wait_ge(T.sem[s["sem"]], s["inc"])
+        if i == BANKS:
+            for k in early:
+                if early[k]:
+                    g.tensor.wait_ge(T.sem["e%d" % k], early[k])
+        hi = s["o"] + s["w"]
+        lo = min(s["o"], hi - NC)
+        bank = T["p%d" % (i % BANKS)]
+        g.tensor.matmul_mx(bank[:, 0:hi - lo], T.wq[:], T.ws[:], T.xq[:, lo:hi], T.xs[:, lo:hi], True, True).then_inc(T.sem["m%d" % i], 1)
+        on_scalar = i % 2 == len(prods) % 2
+        (g.scalar if on_scalar else g.vector).wait_ge(T.sem["m%d" % i], 1)
         for k in range(K):
-            f = (e - k) % n
-            for x in sl:
-                j, c = x["j"], cnt[x["j"]][f]
-                if not c:
-                    continue
-                o = win[j][e][0] + sum(cnt[j][(e - m) % n] for m in range(k + 1, K)) - x["a"] + x["o"] - lo
-                to = k * NC + sum(cnt[i2][f] for i2 in range(j))
-                part = "early" if i < 3 else "f%d" % k
-                done[part] = done.get(part, 0) + 1
-                if on_scalar:
-                    g.scalar.activation(T.ys[:, to:to + c], T[bank][:, o:o + c], ActivationFunctionType.Copy).then_inc(T.sem[part], 1)
-                else:
-                    g.vector.tensor_copy(T.ys[:, to:to + c], T[bank][:, o:o + c]).then_inc(T.sem[part], 1)
-    st = 0
-    for part in (True, False):
-        js = [j for j in range(n) if (topo.host(cores[j]) == topo.host(core)) == part]
-        for k in range(K):
-            f = (e - k) % n
-            lo = k * NC + sum(cnt[j][f] for j in range(js[0]))
-            hi = lo + sum(cnt[j][f] for j in js)
-            if hi == lo:
+            j, f = s["j"], (e - k) % n
+            c = cnt[j][f]
+            if not c:
                 continue
-            if part and not st:
-                g.sync.wait_ge(T.sem.early, done["early"])
-            if not part:
-                g.sync.wait_ge(T.sem["f%d" % k], done["f%d" % k])
-            g.sync.dma_start(T.y[:, lo:hi], T.ys[:, lo:hi]).then_inc(T.sem.st, 16)
-            st += 16
-    g.sync.wait_ge(T.sem.st, st)
+            o = win[j][e][0] + sum(cnt[j][(e - m) % n] for m in range(k + 1, K)) - s["a"] + s["o"] - lo
+            to = k * NC + sum(cnt[i2][f] for i2 in range(j))
+            sem = T.sem[home[j, k]]
+            if on_scalar:
+                g.scalar.activation(T.ys[:, to:to + c], bank[:, o:o + c], ActivationFunctionType.Copy).then_inc(sem, 1)
+            else:
+                g.vector.tensor_copy(T.ys[:, to:to + c], bank[:, o:o + c]).then_inc(sem, 1)
+    for i, (ph, k, lo, hi, need) in enumerate(stores):
+        q = g.scalar if ph == stores[-1][0] and (len(stores) - i) % 2 else g.sync
+        for s, c in need:
+            q.wait_ge(T.sem[s], c)
+        q.dma_start(T.y[:, lo:hi], T.ys[:, lo:hi]).then_inc(T.sem.st, 16)
+    g.sync.wait_ge(T.sem.st, 16 * len(stores))

from concourse.bass import DstId, RemoteDMATransfer
from concourse.mybir import dt, ActivationFunctionType

BANKS = 8
SCRATCH = {
    "xt": ("sbuf", [128, 512], "bfloat16"),
    "wt": ("sbuf", [128, 512], "bfloat16"),
    "xq": ("sbuf", [128, 1024], "float8_e4m3fn_x4"),
    "xs": ("sbuf", [128, 1024], "uint8"),
    "wq": ("sbuf", [128, 128], "float8_e4m3fn_x4"),
    "ws": ("sbuf", [128, 128], "uint8"),
    "rq": ("sbuf", [128, 256], "float8_e4m3fn_x4"),
    "rs": ("sbuf", [128, 256], "uint8"),
    "ys": ("sbuf", [128, 512], "float32"),
}
for _i in range(BANKS):
    SCRATCH["p%d" % _i] = ("psum", [128, 512], "float32")
SEMAPHORES = (["ldx", "ldw", "qx", "qy", "qw", "sent", "ra", "st"] + ["a%d" % i for i in range(8)] + ["m%d" % i for i in range(9)]
              + ["t%d" % i for i in range(12)] + ["e%d" % i for i in range(4)])
K, NC, WORLD = 4, 128, 256
BUDGET = 357632
CALL, ROW, BYTE = 0.1, 0.012, 1 / 14000.
ROWC, GAIN, LAG = 0.02, 0.1, 0.3
HOP = 1.0
THIN, THIN0 = 40, 24
CACHE = {}


def bits(mask):
    return [1 << b for b in range(16) if mask >> b & 1]


def partitions(items):
    if not items:
        yield []
        return
    for rest in partitions(items[1:]):
        yield [[items[0]]] + rest
        for i in range(len(rest)):
            yield rest[:i] + [[items[0]] + rest[i]] + rest[i + 1:]


def pack(core, wins, hi, topo):
    masks = {d: topo.mask(core, d) for d in wins}
    few = min(len(bits(m)) for m in masks.values())
    far = [d for d in wins if len(bits(masks[d])) == few]
    alone = [[d] for d in wins if d not in far]
    pool = bits(masks[far[0]])
    best = None
    for part in partitions(sorted(far)):
        cost, groups = 0, []
        for grp in part:
            w = max(wins[d][1] - wins[d][0] for d in grp)
            per = 1
            while 2 * per * len(grp) <= len(pool):
                per *= 2
            cost += CALL + 1e-3 * w * len(grp) + NC / per * (ROW + 4 * w * BYTE)
            groups.append((w, grp, per))
        if best is None or cost < best[0]:
            best = (cost, groups)
    groups = sorted(best[1], key=lambda g: -g[0]) + [(wins[d][1] - wins[d][0], [d], len(pool)) for [d] in alone]
    calls = []
    for w, grp, per in groups:
        used, tr = set(), {}
        for d in sorted(grp):
            free = [b for b in bits(masks[d]) if b not in used and (d in far or b not in pool)][:per]
            used.update(free)
            tr[d] = (min(wins[d][0], hi - w), free)
        calls.append((w, tr))
    return calls


def relay_cores(n, cores, host, win, over, topo):
    pairs = []
    for j in range(n):
        dst = [cores[e] for e in over[j]]
        by = {}
        for c in range(WORLD):
            if (topo.host(c) == topo.host(dst[0]) and topo.same_plane(cores[j], c) and topo.die(c) != topo.die(cores[j])
                    and all(topo.may_write(c, d) for d in dst)):
                by.setdefault((topo.host(c), topo.chip(c)), []).append(c)
        for h, cs in by.items():
            home = sum(win[j][e][1] - win[j][e][0] for e in over[j] if (host[e], topo.chip(cores[e])) == h)
            if len(cs) >= 2:
                pairs.append((-home, h, j, cs[:2]))
    relay, taken = {}, set()
    for home, h, j, cs in sorted(pairs):
        if j not in relay and h not in taken:
            relay[j] = cs
            taken.add(h)
    return relay


def share(slots, local, a, b, most):
    cost = lambda w: NC / 8 * (ROWC + 4 * w * BYTE)
    best = (cost(b - a) + sum(cost(s["w"]) for s in slots if s is not local) - GAIN, None)
    for low in (True, False):
        for p in range(a + 4, b, 4):
            for q in range(p, min(b, p + most + 1), 4):
                one, two = ((p, b), (a, q)) if low else ((a, q), (p, b))
                px, py = [], []
                for s in slots:
                    lo, hi = s["a"], s["a"] + s["w"]
                    if one[0] <= lo and hi <= one[1]:
                        px.append((s, lo, hi))
                    elif two[0] <= lo and hi <= two[1]:
                        py.append((s, lo, hi))
                    elif low:
                        px.append((s, q, hi))
                        py.append((s, lo, q))
                    else:
                        px.append((s, lo, p))
                        py.append((s, p, hi))
                if any(y <= x for s, x, y in px + py):
                    continue
                t1 = cost(one[1] - one[0])
                t2 = t1 + cost((b - a) / 4) + cost(two[1] - two[0]) + sum(cost(y - x) for s, x, y in py)
                t1 += sum(cost(y - x) for s, x, y in px if s is not local)
                v = max(t1, t2 - LAG) + .1 * t2 + .002 * (q - p)
                if v < best[0]:
                    best = (v, (one, two, px, py, q - p))
    return best[1]


def plan(T, topo):
    if CACHE:
        return CACHE
    P = CACHE
    cnt, cores = T.tables["CNT"], T.cores
    n = len(cores)
    host = [topo.host(c) for c in cores]
    rank = {c: i for i, c in enumerate(cores)}
    spot = lambda c: (topo.host(c), topo.chip(c))
    P["head"], P["win"] = [], []
    for j in range(n):
        other = [e for e in range(n) if host[e] != host[j]]
        mine = [e for e in range(n) if host[e] == host[j]]
        f0 = (min(other) - K + 1) % n
        if max((e - K + 1) % n + K for e in other) <= n:
            f0 = 0
        pos = [sum(cnt[j][(f0 + i) % n] for i in range(m)) for m in range(2 * n + 1)]
        at = {e: (e - K + 1 - f0) % n for e in range(n)}
        tries = []
        for c in range(n - K + 2):
            b = {e: at[e] + n if at[e] < c else at[e] for e in mine}
            tries.append((max(b.values()) - min(b.values()), c, b))
        at.update(min(tries, key=lambda x: x[:2])[2])
        P["head"].append(sum(cnt[j][:f0]) % NC)
        P["win"].append([(pos[at[e]], pos[at[e] + K]) for e in range(n)])
    win = P["win"]
    live = lambda j, e: j != e and win[j][e][1] > win[j][e][0]
    near = [[e for e in range(n) if host[e] == host[j] and live(j, e)] for j in range(n)]
    over = [[e for e in range(n) if host[e] != host[j] and live(j, e)] for j in range(n)]
    calls = P["calls"] = {}
    slots = P["slots"] = {e: [] for e in range(n)}

    def windows(kind, j, groups):
        out = []
        for w, tr in groups:
            r = []
            for d, (a, m) in tr.items():
                s = {"j": j, "a": a, "w": w, "inc": 0, "kind": kind, "t": 0, "to": d}
                slots[rank[d]].append(s)
                r.append((d, m, a, s))
            out.append((w, r))
        return out

    def pieces(core, px, pool):
        by = {}
        for s, x, y in px:
            by.setdefault((spot(s["to"]) == spot(core), x - y), []).append((s["to"], x, s))
        out = []
        for (on, w), ds in sorted(by.items(), key=lambda z: z[0]):
            per = len(pool)
            while per * len(ds) > len(pool):
                per //= 2
            es = [e for e in bits(topo.mask(core, ds[0][0])) if e not in pool] if on else pool
            out.append((-w, [(d, es[i * per:(i + 1) * per], x, s) for i, (d, x, s) in enumerate(ds)]))
        return out

    def send(core, wait, bufs, base, wins, t):
        free = {}
        for w, tr in wins:
            calls.setdefault(core, []).append((wait, bufs, base, [(d, m, a, s, w) for d, m, a, s in tr]))
            t += CALL
            for d, m, a, s in tr:
                end = max([t] + [free.get(x, 0) for x in m]) + NC / len(m) * (ROW + (4 if bufs[0][1] == "q" else 1) * w * BYTE)
                for x in m:
                    free[x] = end
                if isinstance(s, dict):
                    s["inc"] += len(m)
                    s["t"] = max(s["t"], end)
        return max(free.values())

    relay = relay_cores(n, cores, host, win, over, topo)
    prep = {}
    for j in range(n):
        me = cores[j]
        a, b = min(win[j][e][0] for e in over[j]), max(win[j][e][1] for e in over[j])
        m = bits(topo.mask(me, relay[j][0]))
        cw = windows("c", j, pack(relay[j][0], {cores[e]: win[j][e] for e in over[j]}, b, topo))
        bw = windows("b", j, pack(me, {cores[e]: win[j][e] for e in near[j]}, 2 * NC, topo))
        helper = next(c for c in range(WORLD) if c != me and spot(c) == spot(me)
                      and topo.die(c) == topo.die(me) and all(topo.may_write(c, cores[e]) for e in near[j]))
        hm = [x for x in bits(topo.mask(me, helper)) if x not in m][:len(m)]
        lo, hi = min(a for w, tr in bw for d, x, a, s in tr), max(a + w for w, tr in bw for d, x, a, s in tr)
        w = max(b - a, hi - lo)
        prep[j] = (a, b, m, cw, bw, helper, hm, min(lo, 2 * NC - w), w)
    spare = {h: BUDGET - sum(4 * NC * (p[1] - p[0]) + NC * p[-1] for j, p in prep.items() if host[j] != h) for h in set(host)}
    used = set(spot(c) for c in cores) | set(spot(c) for r in relay.values() for c in r)
    load = lambda j: sum(win[j][e][1] - win[j][e][0] for e in over[j]) - max(win[j][e][1] - win[j][e][0] for e in over[j])
    for j in sorted(range(n), key=lambda j: -load(j)):
        me = cores[j]
        a, b, m, cw, bw, helper, hm, lo, w = prep[j]
        h = topo.host(relay[j][0])
        sl = [s for x, tr in cw for d, y, c, s in tr]
        local = next((s for s in sl if spot(s["to"]) == spot(relay[j][0])), None)
        two = share(sl, local, a, b, max(0, spare[h] // (4 * NC)))
        a1, b1, first = a, b, cw
        if two:
            (a1, b1), (a2, b2), px, py, both = two
            spare[h] -= 4 * NC * both
            third = next(c for c in range(WORLD) if topo.host(c) == h and spot(c) not in used and topo.same_plane(me, c)
                         and topo.die(c) == topo.die(me) and all(topo.may_write(c, s["to"]) for s in sl))
            used.add(spot(third))
            first = pieces(relay[j][0], px, m)
        t = send(me, ("qx" if b <= NC else "qy", 1), ("xq", "rq"), 0, [(b1 - a1, [(relay[j][0], m, a1, "ra")])], 0)
        u = v = send(me, ("qy", 1), ("xs", "rs"), 0, [(w, [(relay[j][1], m, a, "ra"), (helper, hm, lo, "ra")])], t)
        if two:
            v = send(me, ("qy", 1), ("xq", "rq"), 0, [(b2 - a2, [(third, m, a2, "ra")])], u)
            send(third, ("ra", len(m)), ("rq", "xq"), a2, pieces(third, py, m), v + HOP)
        send(me, ("qy", 1), ("xq", "xq"), 0, bw, v)
        send(helper, ("ra", len(hm)), ("rs", "xs"), lo, bw, u + HOP)
        send(relay[j][0], ("ra", len(m)), ("rq", "xq"), a1, first, t + HOP)
        send(relay[j][1], ("ra", len(m)), ("rs", "xs"), a, cw, u + HOP)
    for e, sl in slots.items():
        sl.sort(key=lambda s: (s["kind"], s["t"]))
        o = 2 * NC
        for i, s in enumerate(sl):
            s["o"], s["sem"] = o, "a%d" % i
            o += s["w"]
    return P


def remote_calls(g, T, topo, core, P):
    sent, last = 0, None
    for wait, (src, dst), base, tr in P["calls"].get(core, []):
        if wait != last:
            g.wait_ge(T.sem[wait[0]], wait[1])
            last = wait
        ts = []
        for d, m, a, s, w in tr:
            rid, pid = topo.addr(d, core)
            o, sem = (s["o"] + a - s["a"], s["sem"]) if isinstance(s, dict) else (0, s)
            f, t = T[src][:, a - base:a - base + w], T[dst][:, o:o + w]
            if src in ("xq", "rq"):
                f, t = f.bitcast(dt.uint8), t.bitcast(dt.uint8)
            ts.append(RemoteDMATransfer(dst_ids=[DstId(rid=rid, pnc=pid)], dma_engine_mask=sum(m), remote_sem=T.sem[sem], src=f, dst=t))
            sent += len(m)
        g.remote_dma_fused(ts, local_sem=T.sem.sent)
    if sent:
        g.wait_ge(T.sem.sent, sent)


def rank_program(g, core, T, topo):
    e = T.rank_of(core)
    P = plan(T, topo)
    if e is None:
        remote_calls(g, T, topo, core, P)
        return
    cnt, win = T.tables["CNT"], P["win"]
    n = len(T.cores)
    head = P["head"][e]
    g.sync.dma_start(T.xt[:, 0:4 * (NC - head)], T.x[:, 4 * head:4 * NC]).then_inc(T.sem.ldx, 16)
    if head:
        g.scalar.dma_start(T.xt[:, 4 * (NC - head):4 * NC], T.x[:, 0:4 * head]).then_inc(T.sem.ldx, 16)
    loaded = 32 if head else 16
    g.sync.wait_ge(T.sem.ldx, loaded)
    g.sync.dma_start(T.wt[:], T.w[:]).then_inc(T.sem.ldw, 16)
    g.vector.wait_ge(T.sem.ldx, loaded)
    g.vector.quantize_mx(T.xq[:, 0:NC], T.xs[:, 0:NC], T.xt[:]).then_inc(T.sem.qx, 1)
    g.vector.quantize_mx(T.xq[:, NC:2 * NC], T.xs[:, NC:2 * NC], T.xt[:]).then_inc(T.sem.qy, 1)
    g.vector.wait_ge(T.sem.ldw, 16)
    g.vector.quantize_mx(T.wq[:], T.ws[:], T.wt[:]).then_inc(T.sem.qw, 1)
    remote_calls(g, T, topo, core, P)
    sl = P["slots"][e]
    when = {s["j"]: s["t"] for s in sl if s["kind"] == "c"}
    late = sorted(when)
    mine = [j for j in range(n) if j not in when]
    beside = min(late) if min(late) > min(mine) else max(late)
    cuts = []
    for c in range(1, len(late)):
        for ea in (late[:c], late[c:]):
            cuts.append((max(when[j] for j in ea) + .1 * abs(len(ea) - len(late) / 2), ea))
    first = min(cuts)[1]
    stores, home, early = [], {}, {}
    for k in range(K):
        f = (e - k) % n
        size = lambda js: sum(cnt[j][f] for j in js)
        early[k] = sum(1 for j in mine if cnt[j][f])
        part = {j: 1 if size(first) >= THIN and j in first else 2 for j in late}
        part.update({j: 0 if size(mine) >= THIN0 else part[beside] for j in mine})
        for ph in (0, 1, 2):
            js = [j for j in range(n) if cnt[j][f] and part[j] == ph]
            if js:
                sem = "t%d" % len(stores)
                for j in js:
                    home[j, k] = sem if j in when else "e%d" % k
                need = [("e%d" % k, early[k])] if any(j in mine for j in js) else []
                if any(j in when for j in js):
                    need.append((sem, sum(1 for j in js if j in when)))
                lo = k * NC + sum(cnt[j][f] for j in range(js[0]))
                stores.append((ph, k, lo, lo + size(js), need))
    stores.sort(key=lambda s: s[:2])
    own = min(win[e][e][0], NC)
    prods = [{"j": e, "a": own, "o": own, "w": NC}] + sl
    g.tensor.wait_ge(T.sem.qx, 1)
    g.tensor.wait_ge(T.sem.qy, 1)
    g.tensor.wait_ge(T.sem.qw, 1)
    for i, s in enumerate(prods):
        if i:
            g.tensor.wait_ge(T.sem[s["sem"]], s["inc"])
        if i == BANKS:
            for k in early:
                if early[k]:
                    g.tensor.wait_ge(T.sem["e%d" % k], early[k])
        hi = s["o"] + s["w"]
        lo = min(s["o"], hi - NC)
        bank = T["p%d" % (i % BANKS)]
        g.tensor.matmul_mx(bank[:, 0:hi - lo], T.wq[:], T.ws[:], T.xq[:, lo:hi], T.xs[:, lo:hi], True, True).then_inc(T.sem["m%d" % i], 1)
        on_scalar = i % 2 == len(prods) % 2
        (g.scalar if on_scalar else g.vector).wait_ge(T.sem["m%d" % i], 1)
        for k in range(K):
            j, f = s["j"], (e - k) % n
            c = cnt[j][f]
            if not c:
                continue
            o = win[j][e][0] + sum(cnt[j][(e - m) % n] for m in range(k + 1, K)) - s["a"] + s["o"] - lo
            to = k * NC + sum(cnt[i2][f] for i2 in range(j))
            sem = T.sem[home[j, k]]
            if on_scalar:
                g.scalar.activation(T.ys[:, to:to + c], bank[:, o:o + c], ActivationFunctionType.Copy).then_inc(sem, 1)
            else:
                g.vector.tensor_copy(T.ys[:, to:to + c], bank[:, o:o + c]).then_inc(sem, 1)
    for i, (ph, k, lo, hi, need) in enumerate(stores):
        q = g.scalar if ph == stores[-1][0] and (len(stores) - i) % 2 else g.sync
        for s, c in need:
            q.wait_ge(T.sem[s], c)
        q.dma_start(T.y[:, lo:hi], T.ys[:, lo:hi]).then_inc(T.sem.st, 16)
    g.sync.wait_ge(T.sem.st, 16 * len(stores))
